import numpy as np
import ml_dtypes


def mxq(x, axis, fmt="e4m3"):
    dtype, down = {"e4m3": (ml_dtypes.float8_e4m3fn, 7), "e5m2": (ml_dtypes.float8_e5m2, 14)}[fmt]
    v = np.moveaxis(np.asarray(x, np.float32).astype(ml_dtypes.bfloat16).astype(np.float64), axis, -1)
    blocks = v.reshape(v.shape[:-1] + (-1, 32))
    amax = np.abs(blocks).max(-1, keepdims=True)
    byte = np.maximum(np.where(amax > 0, np.frexp(amax)[1] - 1 + 127, 0) - down, 1)
    scale = np.exp2(byte - 127.0)
    codes = (blocks / scale).astype(np.float32).astype(dtype).astype(np.float64)
    return np.moveaxis((codes * scale).reshape(v.shape), -1, axis)


WIDE = False


def mx_kscale(k):
    if not WIDE:
        return np.ones(k)
    levels = np.array([10, -10, 5, -5, 0])
    if k % 512:
        return np.exp2(np.random.permutation(np.resize(levels, k // 32))).repeat(32)
    a = np.empty((k // 512, 16))
    for p in range(k // 512):
        a[p, :8] = np.random.permutation(np.resize(levels, 8))
        for g in range(8):
            far = levels[np.abs(levels - a[p, g]) >= 10]
            a[p, g + 8] = far[np.random.randint(len(far))]
    return np.exp2(a.ravel()).repeat(32)


def f64(x):
    return np.asarray(x).astype(np.float64)


def striped(idx):
    return np.tile(idx.reshape(-1, 16).T, (8, 1)).astype(np.uint16)


def unstriped(offs):
    return offs[:16].T.reshape(-1).astype(np.int64)


def pack_weight(w):
    k, n = w.shape
    w = f64(np.asarray(w, np.float32).astype(ml_dtypes.bfloat16)).reshape(k // 32, 32, n)
    amax = np.abs(w).max(1)
    byte = np.clip(np.where(amax > 0, np.frexp(amax)[1] - 1 + 127 - 7, 1), 1, 254)
    scaled = (w * np.exp2(127.0 - byte)[:, None, :]).reshape(k, n).astype(np.float32)
    words = np.ascontiguousarray(scaled.reshape(k // 512, 128, 4, n).transpose(0, 1, 3, 2)).astype(ml_dtypes.float8_e4m3fn).view(np.uint8)
    return words, np.ascontiguousarray(byte.astype(np.uint8).reshape(k // 512, 16, n))


def unpack_weight(words, scales):
    g, p, n, _ = words.shape
    vals = np.ascontiguousarray(words).view(ml_dtypes.float8_e4m3fn).astype(np.float64) * np.repeat(np.exp2(scales.astype(np.float64) - 127.0), 8, axis=1)[..., None]
    return vals.transpose(0, 1, 3, 2).reshape(g * 512, n)


E2M1 = np.array([0.0, 0.5, 1.0, 1.5, 2.0, 3.0, 4.0, 6.0, -0.0, -0.5, -1.0, -1.5, -2.0, -3.0, -4.0, -6.0])


def pack_fp4(w):
    k, n = w.shape
    w = f64(np.asarray(w, np.float32).astype(ml_dtypes.bfloat16)).reshape(k // 32, 32, n)
    amax = np.abs(w).max(1)
    mant, ex = np.frexp(amax / 6.0)
    byte = np.clip(np.where(amax > 0, np.where(mant > 0.5, ex, ex - 1) + 127, 1), 1, 254)
    scaled = (w * np.exp2(127.0 - byte)[:, None, :]).reshape(k, n).astype(np.float32)
    c = np.ascontiguousarray(scaled.reshape(k // 512, 128, 4, n).transpose(0, 1, 3, 2)).astype(ml_dtypes.float4_e2m1fn).view(np.uint8) & 0xF
    words = (c[..., 0::2] | (c[..., 1::2] << 4)).reshape(k // 512, 128, 2 * n)
    return np.ascontiguousarray(words), np.ascontiguousarray(byte.astype(np.uint8).reshape(k // 512, 16, n))


def unpack_fp4(words, scales):
    g, _, n = scales.shape
    words = np.ascontiguousarray(words).reshape(g, 128, n, 2)
    nib = np.empty((g, 128, n, 4), np.uint8)
    nib[..., 0::2] = words & 0xF
    nib[..., 1::2] = words >> 4
    vals = E2M1[nib] * np.repeat(np.exp2(scales.astype(np.float64) - 127.0), 8, axis=1)[..., None]
    return vals.transpose(0, 1, 3, 2).reshape(g * 512, n)


def sigmoid(v):
    return 1.0 / (1.0 + np.exp(-np.maximum(v, -700.0)))


K, T, S, N, H = 512, 2048, 512, 128, 512


def setup_inputs():
    n = np.random.standard_normal
    s = mx_kscale(K)[:, None]
    u = mx_kscale(H)
    packed_xT = pack_weight(n((K, T)) * s)
    packed_w1 = pack_fp4(n((K, H)) / np.sqrt(K) / s)
    packed_w2 = pack_fp4(n((K, H)) / np.sqrt(K) / s)
    packed_w3 = pack_fp4(n((H, N)) / np.sqrt(H) / u[:, None])
    return {
        "x_words": packed_xT[0],
        "x_scales": packed_xT[1],
        "w1_words": packed_w1[0],
        "w1_scales": packed_w1[1],
        "w2_words": packed_w2[0],
        "w2_scales": packed_w2[1],
        "len_": (np.random.uniform(0.5, 1.5, (H, S))).astype(np.float32),
        "unit": (np.random.uniform(0.6, 1.4, (H, 1)) * u[:, None]).astype(np.float32),
        "w3_words": packed_w3[0],
        "w3_scales": packed_w3[1],
        "offs": striped(np.random.permutation(T)[:S]),
        "co": striped(np.random.permutation(S)),
        "if1": striped(np.random.permutation(S)),
    }


def reference(x_words, x_scales, w1_words, w1_scales, w2_words, w2_scales, len_, unit, w3_words, w3_scales, offs, co, if1):
    xq = unpack_weight(x_words, x_scales)[:, unstriped(offs)]
    wt = unpack_fp4(w1_words, w1_scales).T @ xq
    prio = np.log(np.exp(wt) + 1.0)
    pc = prio[:, unstriped(co)]
    sp = unpack_fp4(w2_words, w2_scales).T @ xq
    bias = sigmoid(sp)
    coal = pc * bias
    pi1 = prio[:, unstriped(if1)]
    itf = np.maximum(pi1 - prio, -0.3 * prio)
    gain = prio + 0.5 * coal - (0.8 * itf)
    evic = gain / f64(len_)
    ci = coal[:, unstriped(if1)]
    hid = f64(unit) * (evic * bias - ci)
    return unpack_fp4(w3_words, w3_scales).T @ mxq(hid, 0, "e4m3")

@@ -1,0 +1,183 @@
+from contextlib import ExitStack
+
+import concourse.mybir as mybir
+
+K, T, S, N, H = 512, 2048, 512, 128, 512
+FLOPS = 2 * K * H * S * 2 + 2 * H * N * S
+
+F32 = mybir.dt.float32
+BF16 = mybir.dt.bfloat16
+I32 = mybir.dt.int32
+U32 = mybir.dt.uint32
+U16 = mybir.dt.uint16
+U8 = mybir.dt.uint8
+FP8X4 = mybir.dt.float8_e4m3fn_x4
+FP4X4 = mybir.dt.float4_e2m1fn_x4
+ALU = mybir.AluOpType
+ACT = mybir.ActivationFunctionType
+
+P = 128
+PACK = 4
+WINDOW = S + 16
+HALF = S // 2
+TINY = 2.0 ** -60
+
+
+def tile_picked_yregall_hint_p_kernel(
+    tc, x_words, x_scales, w1_words, w1_scales, w2_words, w2_scales, len_, unit, w3_words, w3_scales, offs, co, if1, out
+):
+    nc = tc.nc
+    with ExitStack() as ctx:
+        lists = ctx.enter_context(tc.tile_pool(name="lists", bufs=1))
+        keep = ctx.enter_context(tc.tile_pool(name="keep", bufs=1))
+        ring = ctx.enter_context(tc.tile_pool(name="ring", bufs=2))
+        psum = ctx.enter_context(tc.psum_pool(name="psum", bufs=1))
+
+        def load_scale_rows(queue, plane, scales):
+            for q in range(4):
+                queue.dma_start(plane[32 * q : 32 * q + 4, :].bitcast(I32), scales[0, 4 * q : 4 * q + 4, :].bitcast(I32))
+
+        offs_sb = lists.tile([P, S // 16], U16, name="offs_sb")
+        co_sb = lists.tile([P, S // 16], U16, name="co_sb")
+        if1_sb = lists.tile([P, S // 16], U16, name="if1_sb")
+
+        xs_all = keep.tile([P, T], U8, name="xs_all")
+        w2s_raw = keep.tile([P, H], U8, name="w2s_raw")
+        w1s_raw = keep.tile([P, H], U8, name="w1s_raw")
+        w3s = keep.tile([P, N], U8, name="w3s", align_bytes=64)
+        for plane in (w2s_raw, xs_all, w1s_raw, w3s):
+            nc.vector.memset(plane[:].bitcast(I32), 0)
+
+        xw_all = keep.tile([P, T], U32, name="xw_all")
+        w2w_raw = keep.tile([P, 2 * H], U8, name="w2w_raw")
+        w1w_raw = keep.tile([P, 2 * H], U8, name="w1w_raw")
+        w3w = keep.tile([P, 2 * N], U8, name="w3w", align_bytes=64)
+        len_sb = keep.tile([P, PACK * S], F32, name="len_sb")
+        unit_sb = keep.tile([P, PACK], F32, name="unit_sb")
+
+        load_scale_rows(nc.scalar, xs_all, x_scales)
+        load_scale_rows(nc.gpsimd, w2s_raw, w2_scales)
+        nc.sync.dma_start(offs_sb[:], offs)
+        nc.sync.dma_start(co_sb[:], co)
+        nc.sync.dma_start(if1_sb[:], if1)
+        nc.sync.dma_start(w2w_raw[:].bitcast(I32), w2_words[0].bitcast(I32))
+        nc.sync.dma_start(len_sb[:], len_.rearrange("(p t) s -> p (t s)", t=PACK))
+        nc.sync.dma_start(xw_all[:].bitcast(I32), x_words[0].rearrange("p c r -> p (c r)").bitcast(I32))
+        load_scale_rows(nc.sync, w1s_raw, w1_scales)
+        nc.gpsimd.dma_start(w1w_raw[:].bitcast(I32), w1_words[0].bitcast(I32))
+        nc.gpsimd.dma_start(unit_sb[:], unit.rearrange("(p t) o -> p (t o)", t=PACK))
+        nc.gpsimd.dma_start(w3w[:].bitcast(I32), w3_words[0].bitcast(I32))
+        load_scale_rows(nc.sync, w3s, w3_scales)
+
+        prio = [keep.tile([P, WINDOW], F32, name="prio%d" % t) for t in range(PACK)]
+        coal = [keep.tile([P, WINDOW], F32, name="coal%d" % t) for t in range(PACK)]
+        for window in prio + coal:
+            nc.vector.memset(window[:, S:], 0.0)
+
+        def deal(words_raw, scales_raw, name):
+            words = keep.tile([P, 2 * H], U8, name=name + "w", align_bytes=64)
+            scales = keep.tile([P, H], U8, name=name + "s", align_bytes=64)
+            nc.vector.tensor_copy(
+                words[:].rearrange("p (t m b) -> p t m b", t=PACK, b=2),
+                words_raw[:].rearrange("p (m t b) -> p t m b", t=PACK, b=2),
+            )
+            nc.vector.tensor_copy(
+                scales[:].rearrange("p (t m) -> p t m", t=PACK), scales_raw[:].rearrange("p (m t) -> p t m", t=PACK)
+            )
+            return words, scales
+
+        xs = keep.tile([P, S], U8, name="xs", align_bytes=64)
+        xw = keep.tile([P, S], U32, name="xw", align_bytes=64)
+        w2w, w2s = deal(w2w_raw, w2s_raw, "w2")
+        nc.vector.tensor_copy(xs[:], xs_all[:].indirect(offs_sb[:]))
+        len_sq = keep.tile([P, PACK * S], F32, name="len_sq")
+        for cols in (slice(0, 2 * S), slice(2 * S, 4 * S)):
+            nc.vector.tensor_tensor(len_sq[:, cols], len_sb[:, cols], len_sb[:, cols], ALU.mult)
+        nc.vector.tensor_copy(xw[:], xw_all[:].indirect(offs_sb[:]))
+        w1w, w1s = deal(w1w_raw, w1s_raw, "w1")
+
+        half_inv = keep.tile([P, PACK * S], F32, name="half_inv")
+        for cols in (slice(0, 2 * S), slice(2 * S, 4 * S)):
+            nc.scalar.activation(half_inv[:, cols], len_sq[:, cols], ACT.Abs_reciprocal_sqrt, scale=4.0)
+
+        def product(words, scales, t, name):
+            bank = psum.tile([P, S], F32, name=name)
+            nc.tensor.matmul_mx(
+                out=bank[:],
+                lhsT=words[:, 2 * P * t : 2 * P * (t + 1)].bitcast(FP4X4),
+                lhsT_scale=scales[:, P * t : P * (t + 1)],
+                rhs=xw[:].bitcast(FP8X4),
+                rhs_scale=xs[:],
+                start=True,
+                stop=True,
+            )
+            return bank
+
+        sp = [product(w2w, w2s, t, "bank%d" % t) for t in range(PACK)]
+        wt = [product(w1w, w1s, t, "bank%d" % (PACK + t)) for t in range(PACK)]
+
+        bias = [keep.tile([P, S], F32, name="bias%d" % t) for t in range(PACK)]
+        sneg = [keep.tile([P, S], F32, name="sneg%d" % t) for t in range(PACK)]
+        for t in range(PACK):
+            nc.scalar.activation(bias[t][:], sp[t][:], ACT.Sigmoid)
+        for t in range(PACK):
+            nc.scalar.activation(sneg[t][:], wt[t][:], ACT.Sigmoid, scale=-1.0)
+
+        unit36 = keep.tile([P, PACK], F32, name="unit36")
+        nc.vector.tensor_scalar(unit36[:], unit_sb[:], 3.6, None, ALU.mult)
+        ratio = [keep.tile([P, S], F32, name="ratio%d" % t) for t in range(PACK)]
+        for t in range(PACK):
+            cols = slice(S * t, S * (t + 1))
+            nc.vector.tensor_tensor(ratio[t][:], half_inv[:, cols], bias[t][:], ALU.mult)
+
+        logs = [keep.tile([P, S], F32, name="logs%d" % t) for t in range(PACK)]
+        for t in range(PACK):
+            nc.scalar.activation(logs[t][:], sneg[t][:], ACT.Ln, bias=TINY)
+        for t in range(PACK):
+            nc.vector.scalar_tensor_tensor(prio[t][:, :S], logs[t][:], -1.0, wt[t][:], ALU.mult, ALU.max)
+
+        evb = keep.tile([P, PACK, S], F32, name="evb")
+        for t in range(PACK):
+            pc = ring.tile([P, S], F32, name="pc")
+            pi1 = ring.tile([P, S], F32, name="pi1")
+            nc.scalar.activation(pc[:], prio[t][:].indirect(co_sb[:]), ACT.Copy)
+            nc.scalar.activation(pi1[:], prio[t][:].indirect(if1_sb[:]), ACT.Copy)
+            top = ring.tile([P, S], F32, name="top")
+            net = ring.tile([P, S], F32, name="net")
+            gain2 = ring.tile([P, S], F32, name="gain2")
+            nc.vector.scalar_tensor_tensor(coal[t][:, :S], pc[:], unit_sb[:, t : t + 1], bias[t][:], ALU.mult, ALU.mult)
+            nc.vector.scalar_tensor_tensor(top[:], prio[t][:, :S], 0.7, pi1[:], ALU.mult, ALU.max)
+            nc.vector.scalar_tensor_tensor(net[:], top[:], -0.8 / 1.8, prio[t][:, :S], ALU.mult, ALU.add)
+            nc.vector.scalar_tensor_tensor(gain2[:], net[:], unit36[:, t : t + 1], coal[t][:, :S], ALU.mult, ALU.add)
+            nc.vector.tensor_tensor(evb[:, t, :], gain2[:], ratio[t][:], ALU.mult)
+
+        for h in range(2):
+            cols = slice(HALF * h, HALF * (h + 1))
+            ci = ring.tile([P, PACK, HALF], F32, name="ci")
+            for t in range(PACK):
+                nc.scalar.activation(
+                    ci[:, t, :], coal[t][:].indirect(if1_sb[:, HALF // 16 * h : HALF // 16 * (h + 1)]), ACT.Copy
+                )
+            hid = ring.tile([P, HALF, PACK], BF16, name="hid", align_bytes=64)
+            nc.vector.tensor_tensor(
+                hid[:].rearrange("p (c i) t -> p c t i", i=4),
+                evb[:, :, cols].rearrange("p t (c i) -> p c t i", i=4),
+                ci[:].rearrange("p t (c i) -> p c t i", i=4),
+                ALU.subtract,
+            )
+            hw = ring.tile([P, HALF], U32, name="hw", align_bytes=64)
+            hs = ring.tile([P, HALF], U8, name="hs", align_bytes=64)
+            nc.vector.quantize_mx(out=hw[:].bitcast(FP8X4), scales=hs[:], in_=hid[:].rearrange("p c t -> p (c t)"))
+            acc = psum.tile([P, S], F32, name="bank%d" % h)
+            nc.tensor.matmul_mx(
+                out=acc[:, :HALF],
+                lhsT=w3w[:].bitcast(FP4X4),
+                lhsT_scale=w3s[:],
+                rhs=hw[:].bitcast(FP8X4),
+                rhs_scale=hs[:],
+                start=True,
+                stop=True,
+            )
+            res = ring.tile([P, HALF], F32, name="res")
+            nc.scalar.copy(res[:], acc[:, :HALF])
+            nc.sync.dma_start(out[:, cols], res[:])

@@ -19,7 +19,8 @@ ACT = mybir.ActivationFunctionType
 P = 128
 PACK = 4
 WINDOW = S + 16
-HALF = S // 2
+CHUNKS = ((0, 256), (256, 128), (384, 128))
+FUSED = 1
 TINY = 2.0 ** -60
 
 
@@ -30,6 +31,8 @@ def tile_picked_yregall_hint_p_kernel(
     with ExitStack() as ctx:
         lists = ctx.enter_context(tc.tile_pool(name="lists", bufs=1))
         keep = ctx.enter_context(tc.tile_pool(name="keep", bufs=1))
+        reused = ctx.enter_context(tc.tile_pool(name="reused", bufs=1))
+        shared = ctx.enter_context(tc.tile_pool(name="shared", bufs=1))
         ring = ctx.enter_context(tc.tile_pool(name="ring", bufs=2))
         psum = ctx.enter_context(tc.psum_pool(name="psum", bufs=1))
 
@@ -43,30 +46,34 @@ def tile_picked_yregall_hint_p_kernel(
 
         xs_all = keep.tile([P, T], U8, name="xs_all")
         w2s_raw = keep.tile([P, H], U8, name="w2s_raw")
-        w1s_raw = keep.tile([P, H], U8, name="w1s_raw")
+        w1s_raw = reused.tile([P, H], U8, name="w1s_raw", offset=0)
         w3s = keep.tile([P, N], U8, name="w3s", align_bytes=64)
-        for plane in (w2s_raw, xs_all, w1s_raw, w3s):
+        for plane in (xs_all, w2s_raw):
             nc.vector.memset(plane[:].bitcast(I32), 0)
+        for plane in (w1s_raw, w3s):
+            nc.gpsimd.memset(plane[:].bitcast(I32), 0)
 
-        xw_all = keep.tile([P, T], U32, name="xw_all")
+        xw_all = shared.tile([P, T], U32, name="xw_all", offset=0, align_bytes=64)
         w2w_raw = keep.tile([P, 2 * H], U8, name="w2w_raw")
-        w1w_raw = keep.tile([P, 2 * H], U8, name="w1w_raw")
+        w1w_raw = reused.tile([P, 2 * H], U8, name="w1w_raw", offset=H)
         w3w = keep.tile([P, 2 * N], U8, name="w3w", align_bytes=64)
-        len_sb = keep.tile([P, PACK * S], F32, name="len_sb")
+        len_sb = [keep.tile([P, 2 * S], F32, name="len_sb%d" % u) for u in range(2)]
         unit_sb = keep.tile([P, PACK], F32, name="unit_sb")
 
-        load_scale_rows(nc.scalar, xs_all, x_scales)
-        load_scale_rows(nc.gpsimd, w2s_raw, w2_scales)
+        nc.sync.dma_start(w2w_raw[:].bitcast(I32), w2_words[0].bitcast(I32))
+        load_scale_rows(nc.sync, xs_all, x_scales)
         nc.sync.dma_start(offs_sb[:], offs)
+        len_rows = len_.rearrange("(p t) s -> p (t s)", t=PACK)
+        for u in range(2):
+            nc.sync.dma_start(len_sb[u][:], len_rows[:, 2 * S * u : 2 * S * (u + 1)])
+        nc.sync.dma_start(xw_all[:].bitcast(I32), x_words[0].rearrange("p c r -> p (c r)").bitcast(I32))
+        load_scale_rows(nc.sync, w2s_raw, w2_scales)
+        nc.sync.dma_start(w1w_raw[:].bitcast(I32), w1_words[0].bitcast(I32))
+        load_scale_rows(nc.sync, w1s_raw, w1_scales)
+        nc.sync.dma_start(unit_sb[:], unit.rearrange("(p t) o -> p (t o)", t=PACK))
         nc.sync.dma_start(co_sb[:], co)
         nc.sync.dma_start(if1_sb[:], if1)
-        nc.sync.dma_start(w2w_raw[:].bitcast(I32), w2_words[0].bitcast(I32))
-        nc.sync.dma_start(len_sb[:], len_.rearrange("(p t) s -> p (t s)", t=PACK))
-        nc.sync.dma_start(xw_all[:].bitcast(I32), x_words[0].rearrange("p c r -> p (c r)").bitcast(I32))
-        load_scale_rows(nc.sync, w1s_raw, w1_scales)
-        nc.gpsimd.dma_start(w1w_raw[:].bitcast(I32), w1_words[0].bitcast(I32))
-        nc.gpsimd.dma_start(unit_sb[:], unit.rearrange("(p t) o -> p (t o)", t=PACK))
-        nc.gpsimd.dma_start(w3w[:].bitcast(I32), w3_words[0].bitcast(I32))
+        nc.sync.dma_start(w3w[:].bitcast(I32), w3_words[0].bitcast(I32))
         load_scale_rows(nc.sync, w3s, w3_scales)
 
         prio = [keep.tile([P, WINDOW], F32, name="prio%d" % t) for t in range(PACK)]
@@ -74,30 +81,36 @@ def tile_picked_yregall_hint_p_kernel(
         for window in prio + coal:
             nc.vector.memset(window[:, S:], 0.0)
 
-        def deal(words_raw, scales_raw, name):
-            words = keep.tile([P, 2 * H], U8, name=name + "w", align_bytes=64)
-            scales = keep.tile([P, H], U8, name=name + "s", align_bytes=64)
+        def deal_words(words, words_raw):
             nc.vector.tensor_copy(
                 words[:].rearrange("p (t m b) -> p t m b", t=PACK, b=2),
                 words_raw[:].rearrange("p (m t b) -> p t m b", t=PACK, b=2),
             )
+
+        def deal_scales(scales, scales_raw):
             nc.vector.tensor_copy(
                 scales[:].rearrange("p (t m) -> p t m", t=PACK), scales_raw[:].rearrange("p (m t) -> p t m", t=PACK)
             )
-            return words, scales
 
         xs = keep.tile([P, S], U8, name="xs", align_bytes=64)
         xw = keep.tile([P, S], U32, name="xw", align_bytes=64)
-        w2w, w2s = deal(w2w_raw, w2s_raw, "w2")
+        w2w = keep.tile([P, 2 * H], U8, name="w2w", align_bytes=64)
+        deal_words(w2w, w2w_raw)
         nc.vector.tensor_copy(xs[:], xs_all[:].indirect(offs_sb[:]))
         len_sq = keep.tile([P, PACK * S], F32, name="len_sq")
-        for cols in (slice(0, 2 * S), slice(2 * S, 4 * S)):
-            nc.vector.tensor_tensor(len_sq[:, cols], len_sb[:, cols], len_sb[:, cols], ALU.mult)
+        for t in range(PACK):
+            rows = len_sb[t // 2][:, S * (t % 2) : S * (t % 2 + 1)]
+            nc.vector.tensor_tensor(len_sq[:, S * t : S * (t + 1)], rows, rows, ALU.mult)
         nc.vector.tensor_copy(xw[:], xw_all[:].indirect(offs_sb[:]))
-        w1w, w1s = deal(w1w_raw, w1s_raw, "w1")
+        w2s = shared.tile([P, H], U8, name="w2s", offset=0, align_bytes=64)
+        w1w = shared.tile([P, 2 * H], U8, name="w1w", offset=H, align_bytes=64)
+        w1s = shared.tile([P, H], U8, name="w1s", offset=3 * H, align_bytes=64)
+        deal_scales(w2s, w2s_raw)
+        deal_words(w1w, w1w_raw)
+        deal_scales(w1s, w1s_raw)
 
         half_inv = keep.tile([P, PACK * S], F32, name="half_inv")
-        for cols in (slice(0, 2 * S), slice(2 * S, 4 * S)):
+        for cols in [slice(S * t, S * (t + 1)) for t in range(PACK)]:
             nc.scalar.activation(half_inv[:, cols], len_sq[:, cols], ACT.Abs_reciprocal_sqrt, scale=4.0)
 
         def product(words, scales, t, name):
@@ -125,10 +138,14 @@ def tile_picked_yregall_hint_p_kernel(
 
         unit36 = keep.tile([P, PACK], F32, name="unit36")
         nc.vector.tensor_scalar(unit36[:], unit_sb[:], 3.6, None, ALU.mult)
-        ratio = [keep.tile([P, S], F32, name="ratio%d" % t) for t in range(PACK)]
+        ratio = reused.tile([P, PACK, S], F32, name="ratio", offset=0)
         for t in range(PACK):
             cols = slice(S * t, S * (t + 1))
-            nc.vector.tensor_tensor(ratio[t][:], half_inv[:, cols], bias[t][:], ALU.mult)
+            nc.vector.tensor_tensor(ratio[:, t, :], half_inv[:, cols], bias[t][:], ALU.mult)
+
+        scaled_bias = [keep.tile([P, S], F32, name="scaled_bias%d" % t) for t in range(FUSED)]
+        for t in range(FUSED):
+            nc.vector.tensor_scalar(scaled_bias[t][:], bias[t][:], unit_sb[:, t : t + 1], None, ALU.mult)
 
         logs = [keep.tile([P, S], F32, name="logs%d" % t) for t in range(PACK)]
         for t in range(PACK):
@@ -137,40 +154,56 @@ def tile_picked_yregall_hint_p_kernel(
             nc.vector.scalar_tensor_tensor(prio[t][:, :S], logs[t][:], -1.0, wt[t][:], ALU.mult, ALU.max)
 
         evb = keep.tile([P, PACK, S], F32, name="evb")
+        gain2 = [None] * PACK
+
+        def weigh(t):
+            nc.vector.tensor_tensor(evb[:, t, :], gain2[t][:], ratio[:, t, :], ALU.mult)
+
         for t in range(PACK):
-            pc = ring.tile([P, S], F32, name="pc")
             pi1 = ring.tile([P, S], F32, name="pi1")
-            nc.scalar.activation(pc[:], prio[t][:].indirect(co_sb[:]), ACT.Copy)
-            nc.scalar.activation(pi1[:], prio[t][:].indirect(if1_sb[:]), ACT.Copy)
             top = ring.tile([P, S], F32, name="top")
             net = ring.tile([P, S], F32, name="net")
-            gain2 = ring.tile([P, S], F32, name="gain2")
-            nc.vector.scalar_tensor_tensor(coal[t][:, :S], pc[:], unit_sb[:, t : t + 1], bias[t][:], ALU.mult, ALU.mult)
-            nc.vector.scalar_tensor_tensor(top[:], prio[t][:, :S], 0.7, pi1[:], ALU.mult, ALU.max)
+            gain2[t] = ring.tile([P, S], F32, name="gain2")
+            nc.scalar.activation(pi1[:], prio[t][:].indirect(if1_sb[:]), ACT.Copy)
+            if t < FUSED:
+                nc.vector.tensor_tensor(coal[t][:, :S], prio[t][:].indirect(co_sb[:]), scaled_bias[t][:], ALU.mult)
+                nc.vector.scalar_tensor_tensor(top[:], prio[t][:, :S], 0.7, pi1[:], ALU.mult, ALU.max)
+            else:
+                pc = ring.tile([P, S], F32, name="pc")
+                nc.scalar.activation(pc[:], prio[t][:].indirect(co_sb[:]), ACT.Copy)
+                nc.vector.scalar_tensor_tensor(top[:], prio[t][:, :S], 0.7, pi1[:], ALU.mult, ALU.max)
+                nc.vector.scalar_tensor_tensor(coal[t][:, :S], pc[:], unit_sb[:, t : t + 1], bias[t][:], ALU.mult, ALU.mult)
             nc.vector.scalar_tensor_tensor(net[:], top[:], -0.8 / 1.8, prio[t][:, :S], ALU.mult, ALU.add)
-            nc.vector.scalar_tensor_tensor(gain2[:], net[:], unit36[:, t : t + 1], coal[t][:, :S], ALU.mult, ALU.add)
-            nc.vector.tensor_tensor(evb[:, t, :], gain2[:], ratio[t][:], ALU.mult)
+            if t > 0:
+                weigh(t - 1)
+            nc.vector.scalar_tensor_tensor(gain2[t][:], net[:], unit36[:, t : t + 1], coal[t][:, :S], ALU.mult, ALU.add)
+        weigh(PACK - 1)
 
-        for h in range(2):
-            cols = slice(HALF * h, HALF * (h + 1))
-            ci = ring.tile([P, PACK, HALF], F32, name="ci")
+        hid = [None] * len(CHUNKS)
+
+        def round_hidden(c):
+            start, width = CHUNKS[c]
+            ci = keep.tile([P, PACK, width], F32, name="ci%d" % c)
             for t in range(PACK):
                 nc.scalar.activation(
-                    ci[:, t, :], coal[t][:].indirect(if1_sb[:, HALF // 16 * h : HALF // 16 * (h + 1)]), ACT.Copy
+                    ci[:, t, :], coal[t][:].indirect(if1_sb[:, start // 16 : (start + width) // 16]), ACT.Copy
                 )
-            hid = ring.tile([P, HALF, PACK], BF16, name="hid", align_bytes=64)
+            hid[c] = keep.tile([P, width, PACK], BF16, name="hid%d" % c, align_bytes=64)
             nc.vector.tensor_tensor(
-                hid[:].rearrange("p (c i) t -> p c t i", i=4),
-                evb[:, :, cols].rearrange("p t (c i) -> p c t i", i=4),
+                hid[c][:].rearrange("p (c i) t -> p c t i", i=4),
+                evb[:, :, start : start + width].rearrange("p t (c i) -> p c t i", i=4),
                 ci[:].rearrange("p t (c i) -> p c t i", i=4),
                 ALU.subtract,
             )
-            hw = ring.tile([P, HALF], U32, name="hw", align_bytes=64)
-            hs = ring.tile([P, HALF], U8, name="hs", align_bytes=64)
-            nc.vector.quantize_mx(out=hw[:].bitcast(FP8X4), scales=hs[:], in_=hid[:].rearrange("p c t -> p (c t)"))
-            acc = psum.tile([P, S], F32, name="bank%d" % h)
+
+        def classify(c):
+            start, width = CHUNKS[c]
+            hw = keep.tile([P, width], U32, name="hw%d" % c, align_bytes=64)
+            hs = keep.tile([P, width], U8, name="hs%d" % c, align_bytes=64)
+            nc.vector.quantize_mx(out=hw[:].bitcast(FP8X4), scales=hs[:], in_=hid[c][:].rearrange("p c t -> p (c t)"))
+            acc = psum.tile([P, S], F32, name="bank%d" % c)
             nc.tensor.matmul_mx(
-                out=acc[:, :HALF],
+                out=acc[:, :width],
                 lhsT=w3w[:].bitcast(FP4X4),
                 lhsT_scale=w3s[:],
                 rhs=hw[:].bitcast(FP8X4),
@@ -178,6 +211,12 @@ def tile_picked_yregall_hint_p_kernel(
                 start=True,
                 stop=True,
             )
-            res = ring.tile([P, HALF], F32, name="res")
-            nc.scalar.copy(res[:], acc[:, :HALF])
-            nc.sync.dma_start(out[:, cols], res[:])
+            res = keep.tile([P, width], F32, name="res%d" % c)
+            nc.scalar.copy(res[:], acc[:, :width])
+            nc.sync.dma_start(out[:, start : start + width], res[:])
+
+        for c in range(len(CHUNKS)):
+            round_hidden(c)
+            if c > 0:
+                classify(c - 1)
+        classify(len(CHUNKS) - 1)

@@ -1,6 +1,7 @@
 from contextlib import ExitStack
 
 import concourse.mybir as mybir
+from concourse.masks import make_identity
 
 K, T, S, N, H = 512, 2048, 512, 128, 512
 FLOPS = 2 * K * H * S * 2 + 2 * H * N * S
@@ -20,7 +21,7 @@ P = 128
 PACK = 4
 WINDOW = S + 16
 CHUNKS = ((0, 256), (256, 128), (384, 128))
-FUSED = 1
+FUSED = 4
 TINY = 2.0 ** -60
 
 
@@ -53,6 +54,9 @@ def tile_picked_yregall_hint_p_kernel(
         for plane in (w1s_raw, w3s):
             nc.gpsimd.memset(plane[:].bitcast(I32), 0)
 
+        ident = keep.tile([P, P], F32, name="ident")
+        make_identity(nc, ident[:])
+
         xw_all = shared.tile([P, T], U32, name="xw_all", offset=0, align_bytes=64)
         w2w_raw = keep.tile([P, 2 * H], U8, name="w2w_raw")
         w1w_raw = reused.tile([P, 2 * H], U8, name="w1w_raw", offset=H)
@@ -66,8 +70,8 @@ def tile_picked_yregall_hint_p_kernel(
         len_rows = len_.rearrange("(p t) s -> p (t s)", t=PACK)
         for u in range(2):
             nc.sync.dma_start(len_sb[u][:], len_rows[:, 2 * S * u : 2 * S * (u + 1)])
-        nc.sync.dma_start(xw_all[:].bitcast(I32), x_words[0].rearrange("p c r -> p (c r)").bitcast(I32))
         load_scale_rows(nc.sync, w2s_raw, w2_scales)
+        nc.sync.dma_start(xw_all[:].bitcast(I32), x_words[0].rearrange("p c r -> p (c r)").bitcast(I32))
         nc.sync.dma_start(w1w_raw[:].bitcast(I32), w1_words[0].bitcast(I32))
         load_scale_rows(nc.sync, w1s_raw, w1_scales)
         nc.sync.dma_start(unit_sb[:], unit.rearrange("(p t) o -> p (t o)", t=PACK))
@@ -101,11 +105,11 @@ def tile_picked_yregall_hint_p_kernel(
         for t in range(PACK):
             rows = len_sb[t // 2][:, S * (t % 2) : S * (t % 2 + 1)]
             nc.vector.tensor_tensor(len_sq[:, S * t : S * (t + 1)], rows, rows, ALU.mult)
-        nc.vector.tensor_copy(xw[:], xw_all[:].indirect(offs_sb[:]))
-        w2s = shared.tile([P, H], U8, name="w2s", offset=0, align_bytes=64)
-        w1w = shared.tile([P, 2 * H], U8, name="w1w", offset=H, align_bytes=64)
-        w1s = shared.tile([P, H], U8, name="w1s", offset=3 * H, align_bytes=64)
+        w2s = keep.tile([P, H], U8, name="w2s", align_bytes=64)
         deal_scales(w2s, w2s_raw)
+        nc.vector.tensor_copy(xw[:], xw_all[:].indirect(offs_sb[:]))
+        w1w = shared.tile([P, 2 * H], U8, name="w1w", offset=0, align_bytes=64)
+        w1s = shared.tile([P, H], U8, name="w1s", offset=2 * H, align_bytes=64)
         deal_words(w1w, w1w_raw)
         deal_scales(w1s, w1s_raw)
 
@@ -141,11 +145,20 @@ def tile_picked_yregall_hint_p_kernel(
         ratio = reused.tile([P, PACK, S], F32, name="ratio", offset=0)
         for t in range(PACK):
             cols = slice(S * t, S * (t + 1))
-            nc.vector.tensor_tensor(ratio[:, t, :], half_inv[:, cols], bias[t][:], ALU.mult)
+            nc.vector.scalar_tensor_tensor(
+                ratio[:, t, :], half_inv[:, cols], unit36[:, t : t + 1], bias[t][:], ALU.mult, ALU.mult
+            )
+        blocks = [slice(P * b, P * (b + 1)) for b in range(PACK)]
+        ratio_t = [keep.tile([P, S], F32, name="ratio_t%d" % t) for t in range(PACK)]
+        for t in range(PACK):
+            turned = psum.tile([P, S], F32, name="bank%d" % t)
+            for block in blocks:
+                nc.tensor.transpose(turned[:, block], ratio[:, t, block], ident[:])
+            nc.vector.tensor_copy(ratio_t[t][:], turned[:])
 
         scaled_bias = [keep.tile([P, S], F32, name="scaled_bias%d" % t) for t in range(FUSED)]
         for t in range(FUSED):
-            nc.vector.tensor_scalar(scaled_bias[t][:], bias[t][:], unit_sb[:, t : t + 1], None, ALU.mult)
+            nc.vector.tensor_scalar(scaled_bias[t][:], bias[t][:], 0.5 / 1.8, None, ALU.mult)
 
         logs = [keep.tile([P, S], F32, name="logs%d" % t) for t in range(PACK)]
         for t in range(PACK):
@@ -153,48 +166,68 @@ def tile_picked_yregall_hint_p_kernel(
         for t in range(PACK):
             nc.vector.scalar_tensor_tensor(prio[t][:, :S], logs[t][:], -1.0, wt[t][:], ALU.mult, ALU.max)
 
-        evb = keep.tile([P, PACK, S], F32, name="evb")
-        gain2 = [None] * PACK
+        back = [psum.tile([P, PACK, P], F32, name="bank%d" % (PACK + b)) for b in range(PACK)]
+        gain_t = [None] * PACK
 
         def weigh(t):
-            nc.vector.tensor_tensor(evb[:, t, :], gain2[t][:], ratio[:, t, :], ALU.mult)
+            evb_t = ring.tile([P, S], F32, name="evb_t")
+            step = PACK if t < PACK - 1 else PACK // 2
+            for first in range(0, PACK, step):
+                cols = slice(P * first, P * (first + step))
+                nc.vector.tensor_tensor(evb_t[:, cols], gain_t[t][:, cols], ratio_t[t][:, cols], ALU.mult)
+                for b in range(first, first + step):
+                    nc.tensor.transpose(back[b][:, t, :], evb_t[:, blocks[b]], ident[:])
 
         for t in range(PACK):
-            pi1 = ring.tile([P, S], F32, name="pi1")
-            top = ring.tile([P, S], F32, name="top")
-            net = ring.tile([P, S], F32, name="net")
-            gain2[t] = ring.tile([P, S], F32, name="gain2")
-            nc.scalar.activation(pi1[:], prio[t][:].indirect(if1_sb[:]), ACT.Copy)
+            pi1 = ring.tile([P, S], F32, name="pi1", bufs=PACK)
+            loss = ring.tile([P, S], F32, name="loss", bufs=PACK)
+            share = ring.tile([P, S], F32, name="share", bufs=PACK)
+            nc.scalar.activation(pi1[:], prio[t][:].indirect(if1_sb[:]), ACT.Copy, scale=-0.8 / 1.8)
             if t < FUSED:
-                nc.vector.tensor_tensor(coal[t][:, :S], prio[t][:].indirect(co_sb[:]), scaled_bias[t][:], ALU.mult)
-                nc.vector.scalar_tensor_tensor(top[:], prio[t][:, :S], 0.7, pi1[:], ALU.mult, ALU.max)
+                nc.vector.tensor_tensor(share[:], prio[t][:].indirect(co_sb[:]), scaled_bias[t][:], ALU.mult)
+                nc.vector.scalar_tensor_tensor(loss[:], prio[t][:, :S], -0.7 * 0.8 / 1.8, pi1[:], ALU.mult, ALU.min)
+                terms = (prio[t], share, loss)
             else:
                 pc = ring.tile([P, S], F32, name="pc")
                 nc.scalar.activation(pc[:], prio[t][:].indirect(co_sb[:]), ACT.Copy)
-                nc.vector.scalar_tensor_tensor(top[:], prio[t][:, :S], 0.7, pi1[:], ALU.mult, ALU.max)
-                nc.vector.scalar_tensor_tensor(coal[t][:, :S], pc[:], unit_sb[:, t : t + 1], bias[t][:], ALU.mult, ALU.mult)
-            nc.vector.scalar_tensor_tensor(net[:], top[:], -0.8 / 1.8, prio[t][:, :S], ALU.mult, ALU.add)
+                nc.vector.scalar_tensor_tensor(loss[:], prio[t][:, :S], -0.7 * 0.8 / 1.8, pi1[:], ALU.mult, ALU.min)
+                nc.vector.scalar_tensor_tensor(share[:], pc[:], 0.5 / 1.8, bias[t][:], ALU.mult, ALU.mult)
+                terms = (prio[t], loss, share)
+            gain_t[t] = psum.tile([P, S], F32, name="bank%d" % t)
+            for n, term in enumerate(terms):
+                for b, block in enumerate(blocks):
+                    nc.tensor.matmul(
+                        gain_t[t][:, block],
+                        term[:, block],
+                        ident[:],
+                        start=(n == 0 and b == 0),
+                        stop=(n == len(terms) - 1 and b == PACK - 1),
+                        is_transpose=True,
+                    )
             if t > 0:
                 weigh(t - 1)
-            nc.vector.scalar_tensor_tensor(gain2[t][:], net[:], unit36[:, t : t + 1], coal[t][:, :S], ALU.mult, ALU.add)
+            nc.gpsimd.tensor_scalar(coal[t][:, :S], share[:], unit36[:, t : t + 1], 0.0, ALU.mult, ALU.add)
         weigh(PACK - 1)
 
         hid = [None] * len(CHUNKS)
+        ci_all = [keep.tile([P, PACK, width], F32, name="ci%d" % c) for c, (start, width) in enumerate(CHUNKS)]
+        for c, (start, width) in enumerate(CHUNKS):
+            for t in range(PACK):
+                nc.scalar.activation(
+                    ci_all[c][:, t, :], coal[t][:].indirect(if1_sb[:, start // 16 : (start + width) // 16]), ACT.Copy
+                )
 
         def round_hidden(c):
             start, width = CHUNKS[c]
-            ci = keep.tile([P, PACK, width], F32, name="ci%d" % c)
-            for t in range(PACK):
-                nc.scalar.activation(
-                    ci[:, t, :], coal[t][:].indirect(if1_sb[:, start // 16 : (start + width) // 16]), ACT.Copy
-                )
+            ci = ci_all[c]
             hid[c] = keep.tile([P, width, PACK], BF16, name="hid%d" % c, align_bytes=64)
-            nc.vector.tensor_tensor(
-                hid[c][:].rearrange("p (c i) t -> p c t i", i=4),
-                evb[:, :, start : start + width].rearrange("p t (c i) -> p c t i", i=4),
-                ci[:].rearrange("p t (c i) -> p c t i", i=4),
-                ALU.subtract,
-            )
+            for first in range(0, width, P):
+                nc.vector.tensor_tensor(
+                    hid[c][:, first : first + P, :].rearrange("p (c i) t -> p c t i", i=4),
+                    back[(start + first) // P][:].rearrange("p t (c i) -> p c t i", i=4),
+                    ci[:, :, first : first + P].rearrange("p t (c i) -> p c t i", i=4),
+                    ALU.subtract,
+                )
 
         def classify(c):
             start, width = CHUNKS[c]

@@ -21,7 +21,7 @@ P = 128
 PACK = 4
 WINDOW = S + 16
 CHUNKS = ((0, 256), (256, 128), (384, 128))
-FUSED = 4
+FUSED = (0, 1, 3)
 TINY = 2.0 ** -60
 
 
@@ -156,8 +156,8 @@ def tile_picked_yregall_hint_p_kernel(
                 nc.tensor.transpose(turned[:, block], ratio[:, t, block], ident[:])
             nc.vector.tensor_copy(ratio_t[t][:], turned[:])
 
-        scaled_bias = [keep.tile([P, S], F32, name="scaled_bias%d" % t) for t in range(FUSED)]
-        for t in range(FUSED):
+        scaled_bias = {t: keep.tile([P, S], F32, name="scaled_bias%d" % t) for t in FUSED}
+        for t in FUSED:
             nc.vector.tensor_scalar(scaled_bias[t][:], bias[t][:], 0.5 / 1.8, None, ALU.mult)
 
         logs = [keep.tile([P, S], F32, name="logs%d" % t) for t in range(PACK)]
@@ -183,7 +183,7 @@ def tile_picked_yregall_hint_p_kernel(
             loss = ring.tile([P, S], F32, name="loss", bufs=PACK)
             share = ring.tile([P, S], F32, name="share", bufs=PACK)
             nc.scalar.activation(pi1[:], prio[t][:].indirect(if1_sb[:]), ACT.Copy, scale=-0.8 / 1.8)
-            if t < FUSED:
+            if t in FUSED:
                 nc.vector.tensor_tensor(share[:], prio[t][:].indirect(co_sb[:]), scaled_bias[t][:], ALU.mult)
                 nc.vector.scalar_tensor_tensor(loss[:], prio[t][:, :S], -0.7 * 0.8 / 1.8, pi1[:], ALU.mult, ALU.min)
                 terms = (prio[t], share, loss)
@@ -210,22 +210,23 @@ def tile_picked_yregall_hint_p_kernel(
         weigh(PACK - 1)
 
         hid = [None] * len(CHUNKS)
-        ci_all = [keep.tile([P, PACK, width], F32, name="ci%d" % c) for c, (start, width) in enumerate(CHUNKS)]
-        for c, (start, width) in enumerate(CHUNKS):
-            for t in range(PACK):
+        ci = keep.tile([P, PACK, S], F32, name="ci")
+        for t in range(PACK):
+            for start, width in CHUNKS if t == PACK - 1 else ((0, S),):
                 nc.scalar.activation(
-                    ci_all[c][:, t, :], coal[t][:].indirect(if1_sb[:, start // 16 : (start + width) // 16]), ACT.Copy
+                    ci[:, t, start : start + width],
+                    coal[t][:].indirect(if1_sb[:, start // 16 : (start + width) // 16]),
+                    ACT.Copy,
                 )
 
         def round_hidden(c):
             start, width = CHUNKS[c]
-            ci = ci_all[c]
             hid[c] = keep.tile([P, width, PACK], BF16, name="hid%d" % c, align_bytes=64)
             for first in range(0, width, P):
                 nc.vector.tensor_tensor(
                     hid[c][:, first : first + P, :].rearrange("p (c i) t -> p c t i", i=4),
                     back[(start + first) // P][:].rearrange("p t (c i) -> p c t i", i=4),
-                    ci[:, :, first : first + P].rearrange("p t (c i) -> p c t i", i=4),
+                    ci[:, :, start + first : start + first + P].rearrange("p t (c i) -> p c t i", i=4),
                     ALU.subtract,
                 )
 

from contextlib import ExitStack

import concourse.mybir as mybir
from concourse.masks import make_identity

K, T, S, N, H = 512, 2048, 512, 128, 512
FLOPS = 2 * K * H * S * 2 + 2 * H * N * S

F32 = mybir.dt.float32
BF16 = mybir.dt.bfloat16
I32 = mybir.dt.int32
U32 = mybir.dt.uint32
U16 = mybir.dt.uint16
U8 = mybir.dt.uint8
FP8X4 = mybir.dt.float8_e4m3fn_x4
FP4X4 = mybir.dt.float4_e2m1fn_x4
ALU = mybir.AluOpType
ACT = mybir.ActivationFunctionType

P = 128
PACK = 4
WINDOW = S + 16
CHUNKS = ((0, 256), (256, 128), (384, 128))
FUSED = (0, 1, 3)
TINY = 2.0 ** -60


def tile_picked_yregall_hint_p_kernel(
    tc, x_words, x_scales, w1_words, w1_scales, w2_words, w2_scales, len_, unit, w3_words, w3_scales, offs, co, if1, out
):
    nc = tc.nc
    with ExitStack() as ctx:
        lists = ctx.enter_context(tc.tile_pool(name="lists", bufs=1))
        keep = ctx.enter_context(tc.tile_pool(name="keep", bufs=1))
        reused = ctx.enter_context(tc.tile_pool(name="reused", bufs=1))
        shared = ctx.enter_context(tc.tile_pool(name="shared", bufs=1))
        ring = ctx.enter_context(tc.tile_pool(name="ring", bufs=2))
        psum = ctx.enter_context(tc.psum_pool(name="psum", bufs=1))

        def load_scale_rows(queue, plane, scales):
            for q in range(4):
                queue.dma_start(plane[32 * q : 32 * q + 4, :].bitcast(I32), scales[0, 4 * q : 4 * q + 4, :].bitcast(I32))

        offs_sb = lists.tile([P, S // 16], U16, name="offs_sb")
        co_sb = lists.tile([P, S // 16], U16, name="co_sb")
        if1_sb = lists.tile([P, S // 16], U16, name="if1_sb")

        xs_all = keep.tile([P, T], U8, name="xs_all")
        w2s_raw = keep.tile([P, H], U8, name="w2s_raw")
        w1s_raw = reused.tile([P, H], U8, name="w1s_raw", offset=0)
        w3s = keep.tile([P, N], U8, name="w3s", align_bytes=64)
        for plane in (xs_all, w2s_raw):
            nc.vector.memset(plane[:].bitcast(I32), 0)
        for plane in (w1s_raw, w3s):
            nc.gpsimd.memset(plane[:].bitcast(I32), 0)

        ident = keep.tile([P, P], F32, name="ident")
        make_identity(nc, ident[:])

        xw_all = shared.tile([P, T], U32, name="xw_all", offset=0, align_bytes=64)
        w2w_raw = keep.tile([P, 2 * H], U8, name="w2w_raw")
        w1w_raw = reused.tile([P, 2 * H], U8, name="w1w_raw", offset=H)
        w3w = keep.tile([P, 2 * N], U8, name="w3w", align_bytes=64)
        len_sb = [keep.tile([P, 2 * S], F32, name="len_sb%d" % u) for u in range(2)]
        unit_sb = keep.tile([P, PACK], F32, name="unit_sb")

        nc.sync.dma_start(w2w_raw[:].bitcast(I32), w2_words[0].bitcast(I32))
        load_scale_rows(nc.sync, xs_all, x_scales)
        nc.sync.dma_start(offs_sb[:], offs)
        len_rows = len_.rearrange("(p t) s -> p (t s)", t=PACK)
        for u in range(2):
            nc.sync.dma_start(len_sb[u][:], len_rows[:, 2 * S * u : 2 * S * (u + 1)])
        load_scale_rows(nc.sync, w2s_raw, w2_scales)
        nc.sync.dma_start(xw_all[:].bitcast(I32), x_words[0].rearrange("p c r -> p (c r)").bitcast(I32))
        nc.sync.dma_start(w1w_raw[:].bitcast(I32), w1_words[0].bitcast(I32))
        load_scale_rows(nc.sync, w1s_raw, w1_scales)
        nc.sync.dma_start(unit_sb[:], unit.rearrange("(p t) o -> p (t o)", t=PACK))
        nc.sync.dma_start(co_sb[:], co)
        nc.sync.dma_start(if1_sb[:], if1)
        nc.sync.dma_start(w3w[:].bitcast(I32), w3_words[0].bitcast(I32))
        load_scale_rows(nc.sync, w3s, w3_scales)

        prio = [keep.tile([P, WINDOW], F32, name="prio%d" % t) for t in range(PACK)]
        coal = [keep.tile([P, WINDOW], F32, name="coal%d" % t) for t in range(PACK)]
        for window in prio + coal:
            nc.vector.memset(window[:, S:], 0.0)

        def deal_words(words, words_raw):
            nc.vector.tensor_copy(
                words[:].rearrange("p (t m b) -> p t m b", t=PACK, b=2),
                words_raw[:].rearrange("p (m t b) -> p t m b", t=PACK, b=2),
            )

        def deal_scales(scales, scales_raw):
            nc.vector.tensor_copy(
                scales[:].rearrange("p (t m) -> p t m", t=PACK), scales_raw[:].rearrange("p (m t) -> p t m", t=PACK)
            )

        xs = keep.tile([P, S], U8, name="xs", align_bytes=64)
        xw = keep.tile([P, S], U32, name="xw", align_bytes=64)
        w2w = keep.tile([P, 2 * H], U8, name="w2w", align_bytes=64)
        deal_words(w2w, w2w_raw)
        nc.vector.tensor_copy(xs[:], xs_all[:].indirect(offs_sb[:]))
        len_sq = keep.tile([P, PACK * S], F32, name="len_sq")
        for t in range(PACK):
            rows = len_sb[t // 2][:, S * (t % 2) : S * (t % 2 + 1)]
            nc.vector.tensor_tensor(len_sq[:, S * t : S * (t + 1)], rows, rows, ALU.mult)
        w2s = keep.tile([P, H], U8, name="w2s", align_bytes=64)
        deal_scales(w2s, w2s_raw)
        nc.vector.tensor_copy(xw[:], xw_all[:].indirect(offs_sb[:]))
        w1w = shared.tile([P, 2 * H], U8, name="w1w", offset=0, align_bytes=64)
        w1s = shared.tile([P, H], U8, name="w1s", offset=2 * H, align_bytes=64)
        deal_words(w1w, w1w_raw)
        deal_scales(w1s, w1s_raw)

        half_inv = keep.tile([P, PACK * S], F32, name="half_inv")
        for cols in [slice(S * t, S * (t + 1)) for t in range(PACK)]:
            nc.scalar.activation(half_inv[:, cols], len_sq[:, cols], ACT.Abs_reciprocal_sqrt, scale=4.0)

        def product(words, scales, t, name):
            bank = psum.tile([P, S], F32, name=name)
            nc.tensor.matmul_mx(
                out=bank[:],
                lhsT=words[:, 2 * P * t : 2 * P * (t + 1)].bitcast(FP4X4),
                lhsT_scale=scales[:, P * t : P * (t + 1)],
                rhs=xw[:].bitcast(FP8X4),
                rhs_scale=xs[:],
                start=True,
                stop=True,
            )
            return bank

        sp = [product(w2w, w2s, t, "bank%d" % t) for t in range(PACK)]
        wt = [product(w1w, w1s, t, "bank%d" % (PACK + t)) for t in range(PACK)]

        bias = [keep.tile([P, S], F32, name="bias%d" % t) for t in range(PACK)]
        sneg = [keep.tile([P, S], F32, name="sneg%d" % t) for t in range(PACK)]
        for t in range(PACK):
            nc.scalar.activation(bias[t][:], sp[t][:], ACT.Sigmoid)
        for t in range(PACK):
            nc.scalar.activation(sneg[t][:], wt[t][:], ACT.Sigmoid, scale=-1.0)

        unit36 = keep.tile([P, PACK], F32, name="unit36")
        nc.vector.tensor_scalar(unit36[:], unit_sb[:], 3.6, None, ALU.mult)
        ratio = reused.tile([P, PACK, S], F32, name="ratio", offset=0)
        for t in range(PACK):
            cols = slice(S * t, S * (t + 1))
            nc.vector.scalar_tensor_tensor(
                ratio[:, t, :], half_inv[:, cols], unit36[:, t : t + 1], bias[t][:], ALU.mult, ALU.mult
            )
        blocks = [slice(P * b, P * (b + 1)) for b in range(PACK)]
        ratio_t = [keep.tile([P, S], F32, name="ratio_t%d" % t) for t in range(PACK)]
        for t in range(PACK):
            turned = psum.tile([P, S], F32, name="bank%d" % t)
            for block in blocks:
                nc.tensor.transpose(turned[:, block], ratio[:, t, block], ident[:])
            nc.vector.tensor_copy(ratio_t[t][:], turned[:])

        scaled_bias = {t: keep.tile([P, S], F32, name="scaled_bias%d" % t) for t in FUSED}
        for t in FUSED:
            nc.vector.tensor_scalar(scaled_bias[t][:], bias[t][:], 0.5 / 1.8, None, ALU.mult)

        logs = [keep.tile([P, S], F32, name="logs%d" % t) for t in range(PACK)]
        for t in range(PACK):
            nc.scalar.activation(logs[t][:], sneg[t][:], ACT.Ln, bias=TINY)
        for t in range(PACK):
            nc.vector.scalar_tensor_tensor(prio[t][:, :S], logs[t][:], -1.0, wt[t][:], ALU.mult, ALU.max)

        back = [psum.tile([P, PACK, P], F32, name="bank%d" % (PACK + b)) for b in range(PACK)]
        gain_t = [None] * PACK

        def weigh(t):
            evb_t = ring.tile([P, S], F32, name="evb_t")
            step = PACK if t < PACK - 1 else PACK // 2
            for first in range(0, PACK, step):
                cols = slice(P * first, P * (first + step))
                nc.vector.tensor_tensor(evb_t[:, cols], gain_t[t][:, cols], ratio_t[t][:, cols], ALU.mult)
                for b in range(first, first + step):
                    nc.tensor.transpose(back[b][:, t, :], evb_t[:, blocks[b]], ident[:])

        for t in range(PACK):
            pi1 = ring.tile([P, S], F32, name="pi1", bufs=PACK)
            loss = ring.tile([P, S], F32, name="loss", bufs=PACK)
            share = ring.tile([P, S], F32, name="share", bufs=PACK)
            nc.scalar.activation(pi1[:], prio[t][:].indirect(if1_sb[:]), ACT.Copy, scale=-0.8 / 1.8)
            if t in FUSED:
                nc.vector.tensor_tensor(share[:], prio[t][:].indirect(co_sb[:]), scaled_bias[t][:], ALU.mult)
                nc.vector.scalar_tensor_tensor(loss[:], prio[t][:, :S], -0.7 * 0.8 / 1.8, pi1[:], ALU.mult, ALU.min)
                terms = (prio[t], share, loss)
            else:
                pc = ring.tile([P, S], F32, name="pc")
                nc.scalar.activation(pc[:], prio[t][:].indirect(co_sb[:]), ACT.Copy)
                nc.vector.scalar_tensor_tensor(loss[:], prio[t][:, :S], -0.7 * 0.8 / 1.8, pi1[:], ALU.mult, ALU.min)
                nc.vector.scalar_tensor_tensor(share[:], pc[:], 0.5 / 1.8, bias[t][:], ALU.mult, ALU.mult)
                terms = (prio[t], loss, share)
            gain_t[t] = psum.tile([P, S], F32, name="bank%d" % t)
            for n, term in enumerate(terms):
                for b, block in enumerate(blocks):
                    nc.tensor.matmul(
                        gain_t[t][:, block],
                        term[:, block],
                        ident[:],
                        start=(n == 0 and b == 0),
                        stop=(n == len(terms) - 1 and b == PACK - 1),
                        is_transpose=True,
                    )
            if t > 0:
                weigh(t - 1)
            nc.gpsimd.tensor_scalar(coal[t][:, :S], share[:], unit36[:, t : t + 1], 0.0, ALU.mult, ALU.add)
        weigh(PACK - 1)

        hid = [None] * len(CHUNKS)
        ci = keep.tile([P, PACK, S], F32, name="ci")
        for t in range(PACK):
            for start, width in CHUNKS if t == PACK - 1 else ((0, S),):
                nc.scalar.activation(
                    ci[:, t, start : start + width],
                    coal[t][:].indirect(if1_sb[:, start // 16 : (start + width) // 16]),
                    ACT.Copy,
                )

        def round_hidden(c):
            start, width = CHUNKS[c]
            hid[c] = keep.tile([P, width, PACK], BF16, name="hid%d" % c, align_bytes=64)
            for first in range(0, width, P):
                nc.vector.tensor_tensor(
                    hid[c][:, first : first + P, :].rearrange("p (c i) t -> p c t i", i=4),
                    back[(start + first) // P][:].rearrange("p t (c i) -> p c t i", i=4),
                    ci[:, :, start + first : start + first + P].rearrange("p t (c i) -> p c t i", i=4),
                    ALU.subtract,
                )

        def classify(c):
            start, width = CHUNKS[c]
            hw = keep.tile([P, width], U32, name="hw%d" % c, align_bytes=64)
            hs = keep.tile([P, width], U8, name="hs%d" % c, align_bytes=64)
            nc.vector.quantize_mx(out=hw[:].bitcast(FP8X4), scales=hs[:], in_=hid[c][:].rearrange("p c t -> p (c t)"))
            acc = psum.tile([P, S], F32, name="bank%d" % c)
            nc.tensor.matmul_mx(
                out=acc[:, :width],
                lhsT=w3w[:].bitcast(FP4X4),
                lhsT_scale=w3s[:],
                rhs=hw[:].bitcast(FP8X4),
                rhs_scale=hs[:],
                start=True,
                stop=True,
            )
            res = keep.tile([P, width], F32, name="res%d" % c)
            nc.scalar.copy(res[:], acc[:, :width])
            nc.sync.dma_start(out[:, start : start + width], res[:])

        for c in range(len(CHUNKS)):
            round_hidden(c)
            if c > 0:
                classify(c - 1)
        classify(len(CHUNKS) - 1)
